import numpy as np
import ml_dtypes


def mxq(x, axis, fmt="e4m3"):
    dtype, down = {"e4m3": (ml_dtypes.float8_e4m3fn, 7), "e5m2": (ml_dtypes.float8_e5m2, 14)}[fmt]
    v = np.moveaxis(np.asarray(x, np.float32).astype(ml_dtypes.bfloat16).astype(np.float64), axis, -1)
    blocks = v.reshape(v.shape[:-1] + (-1, 32))
    amax = np.abs(blocks).max(-1, keepdims=True)
    byte = np.maximum(np.where(amax > 0, np.frexp(amax)[1] - 1 + 127, 0) - down, 1)
    scale = np.exp2(byte - 127.0)
    codes = (blocks / scale).astype(np.float32).astype(dtype).astype(np.float64)
    return np.moveaxis((codes * scale).reshape(v.shape), -1, axis)


WIDE = False


def mx_kscale(k):
    if not WIDE:
        return np.ones(k)
    levels = np.array([10, -10, 5, -5, 0])
    if k % 512:
        return np.exp2(np.random.permutation(np.resize(levels, k // 32))).repeat(32)
    a = np.empty((k // 512, 16))
    for p in range(k // 512):
        a[p, :8] = np.random.permutation(np.resize(levels, 8))
        for g in range(8):
            far = levels[np.abs(levels - a[p, g]) >= 10]
            a[p, g + 8] = far[np.random.randint(len(far))]
    return np.exp2(a.ravel()).repeat(32)


def f64(x):
    return np.asarray(x).astype(np.float64)


def striped(idx):
    return np.tile(idx.reshape(-1, 16).T, (8, 1)).astype(np.uint16)


def unstriped(offs):
    return offs[:16].T.reshape(-1).astype(np.int64)

def planes(y):
    n, m = y.shape
    v = y.astype(np.float32).astype(ml_dtypes.bfloat16).astype(np.float64).reshape(n // 32, 32, m)
    top = np.abs(v).max(1)
    byte = np.clip(np.where(top > 0, np.frexp(top)[1] - 1 + 127 - 7, 1), 1, 254)
    codes = (v * np.exp2(127.0 - byte)[:, None, :]).reshape(n, m).astype(np.float32).astype(ml_dtypes.float8_e4m3fn).view(np.uint8)
    words = codes.reshape(n // 512, 128, 4, m).transpose(0, 1, 3, 2)
    return np.ascontiguousarray(words), np.ascontiguousarray(byte.astype(np.uint8).reshape(n // 512, 16, m))


K, T, S, V, N, U = 512, 1024, 512, 256, 512, 512


def setup_inputs():
    n = np.random.standard_normal
    s = mx_kscale(K)[:, None]
    return {
        "xT": (n((K, T)) * s).astype(np.float32),
        "w1": (n((K, N)) / np.sqrt(2 * K) / s).astype(np.float32),
        "w2": (n((K, N)) / np.sqrt(2 * K) / s).astype(np.float32),
        "offs": striped(np.random.permutation(T)[:S]),
        "to1": striped(np.random.permutation(U)[:V]),
        "to2": striped(np.random.permutation(U)[:V]),
    }


def reference(xT, w1, w2, offs, to1, to2):
    xq = mxq(f64(xT)[:, unstriped(offs)], 0, "e4m3")
    o0 = np.zeros((N, S))
    o0[:, unstriped(to1)] = mxq(f64(w1), 0, "e4m3").T @ xq[:, :V]
    o1 = np.zeros((N, S))
    o1[:, unstriped(to2)] = mxq(f64(w2), 0, "e4m3").T @ xq[:, V:2 * V]
    out_0 = o0 + o1
    return (out_0,) + planes(out_0)

@@ -1,0 +1,172 @@
+from contextlib import ExitStack
+
+import concourse.mybir as mybir
+
+K, T, V, N, U = 512, 1024, 256, 512, 512
+TAPS = 2
+FLOPS = 2 * TAPS * K * N * V
+
+F32 = mybir.dt.float32
+BF16 = mybir.dt.bfloat16
+U32 = mybir.dt.uint32
+I32 = mybir.dt.int32
+U16 = mybir.dt.uint16
+U8 = mybir.dt.uint8
+FP8X4 = mybir.dt.float8_e4m3fn_x4
+COPY = mybir.ActivationFunctionType.Copy
+ADD = mybir.AluOpType.add
+
+P = 128
+PACK = 4
+LIST_COLS = V // 16
+
+
+def tile_picked_spconv_none_lo_kernel(
+    tc, xT, w1, w2, offs, to1, to2, out_0, out_1, out_2
+):
+    nc = tc.nc
+    with ExitStack() as ctx:
+        sb = ctx.enter_context(tc.tile_pool(name="sb", bufs=1))
+        psum = ctx.enter_context(tc.psum_pool(name="psum", bufs=1))
+
+        offs_sb = sb.tile([P, TAPS * LIST_COLS], U16, name="offs_sb")
+        to_sb = [sb.tile([P, LIST_COLS], U16, name=f"to_sb{d}") for d in range(TAPS)]
+        x_planes = [sb.tile([P, T], F32, name=f"x_plane{j}") for j in range(PACK)]
+        w_raw = [[sb.tile([P, 2, N], F32, name=f"w_raw{d}_{h}") for h in range(2)] for d in range(TAPS)]
+        x_rows = xT.rearrange("(p j) c -> p j c", j=PACK)
+        w_rows = [w.rearrange("(p j) c -> p j c", j=PACK) for w in (w1, w2)]
+
+        nc.sync.dma_start(x_planes[0][:], x_rows[:, 0, :])
+        nc.sync.dma_start(offs_sb[:], offs)
+        for j in range(1, PACK):
+            nc.sync.dma_start(x_planes[j][:], x_rows[:, j, :])
+        for d, to in enumerate((to1, to2)):
+            nc.sync.dma_start(to_sb[d][:], to)
+            for h in range(2):
+                nc.sync.dma_start(w_raw[d][h][:], w_rows[d][:, 2 * h : 2 * h + 2, :])
+
+        windows = [[sb.tile([P, U], F32, name=f"window{d}_{t}") for t in range(PACK)] for d in range(TAPS)]
+        for d in range(TAPS):
+            for t in range(PACK):
+                nc.vector.memset(windows[d][t][:], 0.0)
+
+        picked = [sb.tile([P, PACK, V], BF16, name=f"picked{d}") for d in range(TAPS)]
+        for j in range(PACK):
+            nc.vector.tensor_copy(picked[0][:, j, :], x_planes[j][:].indirect(offs_sb[:, 0:LIST_COLS]))
+            nc.scalar.activation(picked[1][:, j, :], x_planes[j][:].indirect(offs_sb[:, LIST_COLS : 2 * LIST_COLS]), COPY)
+
+        w_grouped = [sb.tile([P, PACK, P, PACK], BF16, name=f"w_grouped{d}", align_bytes=64) for d in range(TAPS)]
+        w_codes = [sb.tile([P, N], U32, name=f"w_codes{d}", align_bytes=64) for d in range(TAPS)]
+        w_scales = [sb.tile([P, N], U8, name=f"w_scales{d}", align_bytes=64) for d in range(TAPS)]
+        x_grouped = [sb.tile([P, V, PACK], BF16, name=f"x_grouped{d}", align_bytes=64) for d in range(TAPS)]
+        x_codes = [sb.tile([P, V], U32, name=f"x_codes{d}", align_bytes=64) for d in range(TAPS)]
+        x_scales = [sb.tile([P, V], U8, name=f"x_scales{d}", align_bytes=64) for d in range(TAPS)]
+        banks = [[psum.tile([P, V], F32, name=f"bank{d}_{t}") for t in range(PACK)] for d in range(TAPS)]
+        staged = [[sb.tile([P, V], F32, name=f"staged{d}_{t}") for t in range(PACK)] for d in range(TAPS)]
+        total = sb.tile([P, PACK, U], F32, name="total")
+        out_grouped = sb.tile([P, U, PACK], BF16, name="out_grouped", align_bytes=64)
+        out_codes = sb.tile([P, U], U32, name="out_codes", align_bytes=64)
+        out_scales = sb.tile([P, U], U8, name="out_scales", align_bytes=64)
+        out_rows = out_0.rearrange("(p t) c -> p t c", t=PACK)
+
+        def group_x(d, copy):
+            copy(
+                x_grouped[d][:].rearrange("p (c i) j -> p c j i", i=4),
+                picked[d][:].rearrange("p j (c i) -> p c j i", i=4),
+            )
+
+        def quantize_x(d):
+            nc.vector.quantize_mx(
+                out=x_codes[d][:].bitcast(FP8X4), scales=x_scales[d][:], in_=x_grouped[d][:].rearrange("p c j -> p (c j)")
+            )
+
+        def group_w(d, h):
+            nc.vector.tensor_copy(
+                w_grouped[d][:, :, :, 2 * h : 2 * h + 2].rearrange("p t m j -> p m j t"),
+                w_raw[d][h][:].rearrange("p j (m t) -> p m j t", t=PACK),
+            )
+
+        def quantize_w(d, t0, t1):
+            cols = slice(t0 * P, t1 * P)
+            nc.vector.quantize_mx(
+                out=w_codes[d][:, cols].bitcast(FP8X4),
+                scales=w_scales[d][:, cols],
+                in_=w_grouped[d][:, t0:t1, :, :].rearrange("p t m j -> p (t m j)"),
+            )
+
+        def multiply(d, t):
+            cols = slice(t * P, (t + 1) * P)
+            nc.tensor.matmul_mx(
+                out=banks[d][t][:],
+                lhsT=w_codes[d][:, cols].bitcast(FP8X4),
+                lhsT_scale=w_scales[d][:, cols],
+                rhs=x_codes[d][:].bitcast(FP8X4),
+                rhs_scale=x_scales[d][:],
+                start=True,
+                stop=True,
+            )
+
+        def place_on_vector(d, t):
+            nc.vector.tensor_copy(staged[d][t][:], banks[d][t][:])
+            nc.vector.tensor_copy(windows[d][t][:].indirect(to_sb[d][:]), staged[d][t][:])
+
+        def place_on_scalar(d, t):
+            nc.scalar.copy(staged[d][t][:], banks[d][t][:])
+            nc.scalar.activation(windows[d][t][:].indirect(to_sb[d][:]), staged[d][t][:], COPY)
+
+        def add_taps(t, engine):
+            engine.tensor_tensor(total[:, t, :], windows[0][t][:], windows[1][t][:], ADD)
+            nc.sync.dma_start(out_rows[:, t, :], total[:, t, :])
+
+        def group_out(cols, copy):
+            copy(
+                out_grouped[:, cols, :].rearrange("p (c i) t -> p c t i", i=4),
+                total[:, :, cols].rearrange("p t (c i) -> p c t i", i=4),
+            )
+
+        def quantize_out(cols):
+            nc.vector.quantize_mx(
+                out=out_codes[:, cols].bitcast(FP8X4),
+                scales=out_scales[:, cols],
+                in_=out_grouped[:, cols, :].rearrange("p c t -> p (c t)"),
+            )
+            nc.sync.dma_start(
+                out_1[0].rearrange("p c r -> p (c r)").bitcast(I32)[:, cols], out_codes[:, cols].bitcast(I32)
+            )
+
+        group_x(0, nc.vector.tensor_copy)
+        group_x(1, nc.scalar.copy)
+        group_w(0, 0)
+        quantize_x(0)
+        quantize_x(1)
+        group_w(0, 1)
+        quantize_w(0, 0, 1)
+        quantize_w(0, 1, 2)
+        quantize_w(0, 2, 4)
+        for t in range(PACK):
+            multiply(0, t)
+        place_on_scalar(0, 0)
+        place_on_vector(0, 1)
+        place_on_scalar(0, 2)
+        group_w(1, 0)
+        group_w(1, 1)
+        quantize_w(1, 0, 1)
+        quantize_w(1, 1, 4)
+        for t in range(PACK):
+            multiply(1, t)
+        place_on_scalar(0, 3)
+        place_on_vector(1, 0)
+        place_on_scalar(1, 1)
+        place_on_vector(1, 2)
+        place_on_scalar(1, 3)
+        for t in range(PACK):
+            add_taps(t, nc.vector)
+        halves = (slice(0, U // 2), slice(U // 2, U))
+        group_out(halves[0], nc.scalar.copy)
+        group_out(halves[1], nc.vector.tensor_copy)
+        quantize_out(halves[1])
+        quantize_out(halves[0])
+        scale_rows = out_2[0].bitcast(I32)
+        for q in range(4):
+            queue = nc.scalar if q % 2 else nc.sync
+            queue.dma_start(scale_rows[4 * q : 4 * q + 4, :], out_scales[32 * q : 32 * q + 4, :].bitcast(I32))

@@ -19,6 +19,8 @@ ADD = mybir.AluOpType.add
 P = 128
 PACK = 4
 LIST_COLS = V // 16
+W_SPLIT = 84
+W2_SPLIT = 96
 
 
 def tile_picked_spconv_none_lo_kernel(
@@ -32,7 +34,8 @@ def tile_picked_spconv_none_lo_kernel(
         offs_sb = sb.tile([P, TAPS * LIST_COLS], U16, name="offs_sb")
         to_sb = [sb.tile([P, LIST_COLS], U16, name=f"to_sb{d}") for d in range(TAPS)]
         x_planes = [sb.tile([P, T], F32, name=f"x_plane{j}") for j in range(PACK)]
-        w_raw = [[sb.tile([P, 2, N], F32, name=f"w_raw{d}_{h}") for h in range(2)] for d in range(TAPS)]
+        w1_raw = sb.tile([P, PACK, N], F32, name="w1_raw")
+        w2_raw = [sb.tile([P, 2, N], F32, name=f"w2_raw{h}") for h in range(2)]
         x_rows = xT.rearrange("(p j) c -> p j c", j=PACK)
         w_rows = [w.rearrange("(p j) c -> p j c", j=PACK) for w in (w1, w2)]
 
@@ -40,20 +43,25 @@ def tile_picked_spconv_none_lo_kernel(
         nc.sync.dma_start(offs_sb[:], offs)
         for j in range(1, PACK):
             nc.sync.dma_start(x_planes[j][:], x_rows[:, j, :])
-        for d, to in enumerate((to1, to2)):
-            nc.sync.dma_start(to_sb[d][:], to)
-            for h in range(2):
-                nc.sync.dma_start(w_raw[d][h][:], w_rows[d][:, 2 * h : 2 * h + 2, :])
+        nc.sync.dma_start(w1_raw[:], w_rows[0])
+        nc.sync.dma_start(to_sb[0][:], to1)
+        for h in range(2):
+            nc.sync.dma_start(w2_raw[h][:], w_rows[1][:, 2 * h : 2 * h + 2, :])
+        nc.sync.dma_start(to_sb[1][:], to2)
 
         windows = [[sb.tile([P, U], F32, name=f"window{d}_{t}") for t in range(PACK)] for d in range(TAPS)]
         for d in range(TAPS):
             for t in range(PACK):
-                nc.vector.memset(windows[d][t][:], 0.0)
+                (nc.gpsimd if d else nc.vector).memset(windows[d][t][:], 0.0)
 
         picked = [sb.tile([P, PACK, V], BF16, name=f"picked{d}") for d in range(TAPS)]
         for j in range(PACK):
             nc.vector.tensor_copy(picked[0][:, j, :], x_planes[j][:].indirect(offs_sb[:, 0:LIST_COLS]))
-            nc.scalar.activation(picked[1][:, j, :], x_planes[j][:].indirect(offs_sb[:, LIST_COLS : 2 * LIST_COLS]), COPY)
+            looked_up = x_planes[j][:].indirect(offs_sb[:, LIST_COLS : 2 * LIST_COLS])
+            if j == 1:
+                nc.vector.tensor_copy(picked[1][:, j, :], looked_up)
+            else:
+                nc.scalar.activation(picked[1][:, j, :], looked_up, COPY)
 
         w_grouped = [sb.tile([P, PACK, P, PACK], BF16, name=f"w_grouped{d}", align_bytes=64) for d in range(TAPS)]
         w_codes = [sb.tile([P, N], U32, name=f"w_codes{d}", align_bytes=64) for d in range(TAPS)]
@@ -61,8 +69,17 @@ def tile_picked_spconv_none_lo_kernel(
         x_grouped = [sb.tile([P, V, PACK], BF16, name=f"x_grouped{d}", align_bytes=64) for d in range(TAPS)]
         x_codes = [sb.tile([P, V], U32, name=f"x_codes{d}", align_bytes=64) for d in range(TAPS)]
         x_scales = [sb.tile([P, V], U8, name=f"x_scales{d}", align_bytes=64) for d in range(TAPS)]
-        banks = [[psum.tile([P, V], F32, name=f"bank{d}_{t}") for t in range(PACK)] for d in range(TAPS)]
-        staged = [[sb.tile([P, V], F32, name=f"staged{d}_{t}") for t in range(PACK)] for d in range(TAPS)]
+        bank_of = {}
+        staged = {}
+        groups = [((0, 0),), ((0, 1),), ((1, 0), (1, 1)), ((1, 2), (0, 2)), ((1, 3), (0, 3))]
+        banks = [psum.tile([P, len(g), V], F32, name=f"bank{b}") for b, g in enumerate(groups)]
+        stages = [sb.tile([P, len(g), V], F32, name=f"stage{b}") for b, g in enumerate(groups)]
+        stages[0] = w2_raw[0][:, 0:1, :V]
+        stages[1] = w2_raw[1][:, 0:1, :V]
+        for b, g in enumerate(groups):
+            for s, product in enumerate(g):
+                bank_of[product] = banks[b][:, s, :]
+                staged[product] = stages[b][:, s, :]
         total = sb.tile([P, PACK, U], F32, name="total")
         out_grouped = sb.tile([P, U, PACK], BF16, name="out_grouped", align_bytes=64)
         out_codes = sb.tile([P, U], U32, name="out_codes", align_bytes=64)
@@ -80,10 +97,16 @@ def tile_picked_spconv_none_lo_kernel(
                 out=x_codes[d][:].bitcast(FP8X4), scales=x_scales[d][:], in_=x_grouped[d][:].rearrange("p c j -> p (c j)")
             )
 
-        def group_w(d, h):
-            nc.vector.tensor_copy(
-                w_grouped[d][:, :, :, 2 * h : 2 * h + 2].rearrange("p t m j -> p m j t"),
-                w_raw[d][h][:].rearrange("p j (m t) -> p m j t", t=PACK),
+        def group_w(d, m, raw, copy):
+            copy(
+                w_grouped[d][:, :, m, :].rearrange("p t m j -> p m t j"),
+                raw.rearrange("p j (m t) -> p m t j", t=PACK),
+            )
+
+        def group_w2(h, m, copy):
+            copy(
+                w_grouped[1][:, :, m, 2 * h : 2 * h + 2].rearrange("p t m j -> p m j t"),
+                w2_raw[h][:].rearrange("p j (m t) -> p m j t", t=PACK)[:, m, :, :],
             )
 
         def quantize_w(d, t0, t1):
@@ -97,7 +120,7 @@ def tile_picked_spconv_none_lo_kernel(
         def multiply(d, t):
             cols = slice(t * P, (t + 1) * P)
             nc.tensor.matmul_mx(
-                out=banks[d][t][:],
+                out=bank_of[d, t],
                 lhsT=w_codes[d][:, cols].bitcast(FP8X4),
                 lhsT_scale=w_scales[d][:, cols],
                 rhs=x_codes[d][:].bitcast(FP8X4),
@@ -106,16 +129,19 @@ def tile_picked_spconv_none_lo_kernel(
                 stop=True,
             )
 
-        def place_on_vector(d, t):
-            nc.vector.tensor_copy(staged[d][t][:], banks[d][t][:])
-            nc.vector.tensor_copy(windows[d][t][:].indirect(to_sb[d][:]), staged[d][t][:])
+        def stage(b, copy):
+            copy(stages[b][:, :, :], banks[b][:])
 
-        def place_on_scalar(d, t):
-            nc.scalar.copy(staged[d][t][:], banks[d][t][:])
-            nc.scalar.activation(windows[d][t][:].indirect(to_sb[d][:]), staged[d][t][:], COPY)
+        def scatter_on_vector(d, t, a=0, b=LIST_COLS):
+            nc.vector.tensor_copy(windows[d][t][:].indirect(to_sb[d][:, a:b]), staged[d, t][:, 16 * a : 16 * b])
 
-        def add_taps(t, engine):
-            engine.tensor_tensor(total[:, t, :], windows[0][t][:], windows[1][t][:], ADD)
+        def scatter_on_scalar(d, t, a=0, b=LIST_COLS):
+            nc.scalar.activation(windows[d][t][:].indirect(to_sb[d][:, a:b]), staged[d, t][:, 16 * a : 16 * b], COPY)
+
+        def add_taps(t, cols, engine):
+            engine.tensor_tensor(total[:, t, cols], windows[0][t][:, cols], windows[1][t][:, cols], ADD)
+
+        def store_total(t):
             nc.sync.dma_start(out_rows[:, t, :], total[:, t, :])
 
         def group_out(cols, copy):
@@ -134,38 +160,53 @@ def tile_picked_spconv_none_lo_kernel(
                 out_1[0].rearrange("p c r -> p (c r)").bitcast(I32)[:, cols], out_codes[:, cols].bitcast(I32)
             )
 
-        group_x(0, nc.vector.tensor_copy)
-        group_x(1, nc.scalar.copy)
-        group_w(0, 0)
+        on_vector, on_scalar = nc.vector.tensor_copy, nc.scalar.copy
+        group_x(0, on_vector)
+        group_x(1, on_scalar)
         quantize_x(0)
         quantize_x(1)
-        group_w(0, 1)
+        group_w(0, slice(0, W_SPLIT), w1_raw[:, :, : PACK * W_SPLIT], on_vector)
+        group_w(0, slice(W_SPLIT, P), w1_raw[:, :, PACK * W_SPLIT :], on_scalar)
+        group_w2(0, slice(0, W2_SPLIT), on_scalar)
         quantize_w(0, 0, 1)
         quantize_w(0, 1, 2)
         quantize_w(0, 2, 4)
+        group_w2(0, slice(W2_SPLIT, P), on_vector)
         for t in range(PACK):
             multiply(0, t)
-        place_on_scalar(0, 0)
-        place_on_vector(0, 1)
-        place_on_scalar(0, 2)
-        group_w(1, 0)
-        group_w(1, 1)
-        quantize_w(1, 0, 1)
-        quantize_w(1, 1, 4)
+        stage(0, on_scalar)
+        scatter_on_scalar(0, 0)
+        group_w2(1, slice(0, P), on_vector)
+        quantize_w(1, 0, 2)
+        stage(1, on_vector)
+        quantize_w(1, 2, 4)
+        scatter_on_vector(0, 1)
         for t in range(PACK):
             multiply(1, t)
-        place_on_scalar(0, 3)
-        place_on_vector(1, 0)
-        place_on_scalar(1, 1)
-        place_on_vector(1, 2)
-        place_on_scalar(1, 3)
-        for t in range(PACK):
-            add_taps(t, nc.vector)
-        halves = (slice(0, U // 2), slice(U // 2, U))
-        group_out(halves[0], nc.scalar.copy)
-        group_out(halves[1], nc.vector.tensor_copy)
-        quantize_out(halves[1])
-        quantize_out(halves[0])
+        stage(2, on_scalar)
+        stage(3, on_vector)
+        stage(4, on_scalar)
+        scatter_on_scalar(1, 0)
+        scatter_on_vector(1, 1)
+        scatter_on_scalar(1, 3, 0, 6)
+        scatter_on_scalar(0, 2)
+        scatter_on_vector(1, 2)
+        scatter_on_scalar(0, 3)
+        scatter_on_vector(1, 3, 6, LIST_COLS)
+        for t in range(2):
+            add_taps(t, slice(0, U), nc.gpsimd)
+            store_total(t)
+        add_taps(2, slice(0, U), nc.vector)
+        store_total(2)
+        pieces = (slice(0, 192), slice(U // 2, U), slice(192, U // 2))
+        for piece in pieces:
+            add_taps(3, piece, nc.vector)
+        store_total(3)
+        group_out(pieces[0], on_scalar)
+        group_out(pieces[1], on_vector)
+        group_out(pieces[2], on_vector)
+        quantize_out(slice(U // 2, U))
+        quantize_out(slice(0, U // 2))
         scale_rows = out_2[0].bitcast(I32)
         for q in range(4):
             queue = nc.scalar if q % 2 else nc.sync

from contextlib import ExitStack

import concourse.mybir as mybir

K, T, V, N, U = 512, 1024, 256, 512, 512
TAPS = 2
FLOPS = 2 * TAPS * K * N * V

F32 = mybir.dt.float32
BF16 = mybir.dt.bfloat16
U32 = mybir.dt.uint32
I32 = mybir.dt.int32
U16 = mybir.dt.uint16
U8 = mybir.dt.uint8
FP8X4 = mybir.dt.float8_e4m3fn_x4
COPY = mybir.ActivationFunctionType.Copy
ADD = mybir.AluOpType.add

P = 128
PACK = 4
LIST_COLS = V // 16
W_SPLIT = 84
W2_SPLIT = 96


def tile_picked_spconv_none_lo_kernel(
    tc, xT, w1, w2, offs, to1, to2, out_0, out_1, out_2
):
    nc = tc.nc
    with ExitStack() as ctx:
        sb = ctx.enter_context(tc.tile_pool(name="sb", bufs=1))
        psum = ctx.enter_context(tc.psum_pool(name="psum", bufs=1))

        offs_sb = sb.tile([P, TAPS * LIST_COLS], U16, name="offs_sb")
        to_sb = [sb.tile([P, LIST_COLS], U16, name=f"to_sb{d}") for d in range(TAPS)]
        x_planes = [sb.tile([P, T], F32, name=f"x_plane{j}") for j in range(PACK)]
        w1_raw = sb.tile([P, PACK, N], F32, name="w1_raw")
        w2_raw = [sb.tile([P, 2, N], F32, name=f"w2_raw{h}") for h in range(2)]
        x_rows = xT.rearrange("(p j) c -> p j c", j=PACK)
        w_rows = [w.rearrange("(p j) c -> p j c", j=PACK) for w in (w1, w2)]

        nc.sync.dma_start(x_planes[0][:], x_rows[:, 0, :])
        nc.sync.dma_start(offs_sb[:], offs)
        for j in range(1, PACK):
            nc.sync.dma_start(x_planes[j][:], x_rows[:, j, :])
        nc.sync.dma_start(w1_raw[:], w_rows[0])
        nc.sync.dma_start(to_sb[0][:], to1)
        for h in range(2):
            nc.sync.dma_start(w2_raw[h][:], w_rows[1][:, 2 * h : 2 * h + 2, :])
        nc.sync.dma_start(to_sb[1][:], to2)

        windows = [[sb.tile([P, U], F32, name=f"window{d}_{t}") for t in range(PACK)] for d in range(TAPS)]
        for d in range(TAPS):
            for t in range(PACK):
                (nc.gpsimd if d else nc.vector).memset(windows[d][t][:], 0.0)

        picked = [sb.tile([P, PACK, V], BF16, name=f"picked{d}") for d in range(TAPS)]
        for j in range(PACK):
            nc.vector.tensor_copy(picked[0][:, j, :], x_planes[j][:].indirect(offs_sb[:, 0:LIST_COLS]))
            looked_up = x_planes[j][:].indirect(offs_sb[:, LIST_COLS : 2 * LIST_COLS])
            if j == 1:
                nc.vector.tensor_copy(picked[1][:, j, :], looked_up)
            else:
                nc.scalar.activation(picked[1][:, j, :], looked_up, COPY)

        w_grouped = [sb.tile([P, PACK, P, PACK], BF16, name=f"w_grouped{d}", align_bytes=64) for d in range(TAPS)]
        w_codes = [sb.tile([P, N], U32, name=f"w_codes{d}", align_bytes=64) for d in range(TAPS)]
        w_scales = [sb.tile([P, N], U8, name=f"w_scales{d}", align_bytes=64) for d in range(TAPS)]
        x_grouped = [sb.tile([P, V, PACK], BF16, name=f"x_grouped{d}", align_bytes=64) for d in range(TAPS)]
        x_codes = [sb.tile([P, V], U32, name=f"x_codes{d}", align_bytes=64) for d in range(TAPS)]
        x_scales = [sb.tile([P, V], U8, name=f"x_scales{d}", align_bytes=64) for d in range(TAPS)]
        bank_of = {}
        staged = {}
        groups = [((0, 0),), ((0, 1),), ((1, 0), (1, 1)), ((1, 2), (0, 2)), ((1, 3), (0, 3))]
        banks = [psum.tile([P, len(g), V], F32, name=f"bank{b}") for b, g in enumerate(groups)]
        stages = [sb.tile([P, len(g), V], F32, name=f"stage{b}") for b, g in enumerate(groups)]
        stages[0] = w2_raw[0][:, 0:1, :V]
        stages[1] = w2_raw[1][:, 0:1, :V]
        for b, g in enumerate(groups):
            for s, product in enumerate(g):
                bank_of[product] = banks[b][:, s, :]
                staged[product] = stages[b][:, s, :]
        total = sb.tile([P, PACK, U], F32, name="total")
        out_grouped = sb.tile([P, U, PACK], BF16, name="out_grouped", align_bytes=64)
        out_codes = sb.tile([P, U], U32, name="out_codes", align_bytes=64)
        out_scales = sb.tile([P, U], U8, name="out_scales", align_bytes=64)
        out_rows = out_0.rearrange("(p t) c -> p t c", t=PACK)

        def group_x(d, copy):
            copy(
                x_grouped[d][:].rearrange("p (c i) j -> p c j i", i=4),
                picked[d][:].rearrange("p j (c i) -> p c j i", i=4),
            )

        def quantize_x(d):
            nc.vector.quantize_mx(
                out=x_codes[d][:].bitcast(FP8X4), scales=x_scales[d][:], in_=x_grouped[d][:].rearrange("p c j -> p (c j)")
            )

        def group_w(d, m, raw, copy):
            copy(
                w_grouped[d][:, :, m, :].rearrange("p t m j -> p m t j"),
                raw.rearrange("p j (m t) -> p m t j", t=PACK),
            )

        def group_w2(h, m, copy):
            copy(
                w_grouped[1][:, :, m, 2 * h : 2 * h + 2].rearrange("p t m j -> p m j t"),
                w2_raw[h][:].rearrange("p j (m t) -> p m j t", t=PACK)[:, m, :, :],
            )

        def quantize_w(d, t0, t1):
            cols = slice(t0 * P, t1 * P)
            nc.vector.quantize_mx(
                out=w_codes[d][:, cols].bitcast(FP8X4),
                scales=w_scales[d][:, cols],
                in_=w_grouped[d][:, t0:t1, :, :].rearrange("p t m j -> p (t m j)"),
            )

        def multiply(d, t):
            cols = slice(t * P, (t + 1) * P)
            nc.tensor.matmul_mx(
                out=bank_of[d, t],
                lhsT=w_codes[d][:, cols].bitcast(FP8X4),
                lhsT_scale=w_scales[d][:, cols],
                rhs=x_codes[d][:].bitcast(FP8X4),
                rhs_scale=x_scales[d][:],
                start=True,
                stop=True,
            )

        def stage(b, copy):
            copy(stages[b][:, :, :], banks[b][:])

        def scatter_on_vector(d, t, a=0, b=LIST_COLS):
            nc.vector.tensor_copy(windows[d][t][:].indirect(to_sb[d][:, a:b]), staged[d, t][:, 16 * a : 16 * b])

        def scatter_on_scalar(d, t, a=0, b=LIST_COLS):
            nc.scalar.activation(windows[d][t][:].indirect(to_sb[d][:, a:b]), staged[d, t][:, 16 * a : 16 * b], COPY)

        def add_taps(t, cols, engine):
            engine.tensor_tensor(total[:, t, cols], windows[0][t][:, cols], windows[1][t][:, cols], ADD)

        def store_total(t):
            nc.sync.dma_start(out_rows[:, t, :], total[:, t, :])

        def group_out(cols, copy):
            copy(
                out_grouped[:, cols, :].rearrange("p (c i) t -> p c t i", i=4),
                total[:, :, cols].rearrange("p t (c i) -> p c t i", i=4),
            )

        def quantize_out(cols):
            nc.vector.quantize_mx(
                out=out_codes[:, cols].bitcast(FP8X4),
                scales=out_scales[:, cols],
                in_=out_grouped[:, cols, :].rearrange("p c t -> p (c t)"),
            )
            nc.sync.dma_start(
                out_1[0].rearrange("p c r -> p (c r)").bitcast(I32)[:, cols], out_codes[:, cols].bitcast(I32)
            )

        on_vector, on_scalar = nc.vector.tensor_copy, nc.scalar.copy
        group_x(0, on_vector)
        group_x(1, on_scalar)
        quantize_x(0)
        quantize_x(1)
        group_w(0, slice(0, W_SPLIT), w1_raw[:, :, : PACK * W_SPLIT], on_vector)
        group_w(0, slice(W_SPLIT, P), w1_raw[:, :, PACK * W_SPLIT :], on_scalar)
        group_w2(0, slice(0, W2_SPLIT), on_scalar)
        quantize_w(0, 0, 1)
        quantize_w(0, 1, 2)
        quantize_w(0, 2, 4)
        group_w2(0, slice(W2_SPLIT, P), on_vector)
        for t in range(PACK):
            multiply(0, t)
        stage(0, on_scalar)
        scatter_on_scalar(0, 0)
        group_w2(1, slice(0, P), on_vector)
        quantize_w(1, 0, 2)
        stage(1, on_vector)
        quantize_w(1, 2, 4)
        scatter_on_vector(0, 1)
        for t in range(PACK):
            multiply(1, t)
        stage(2, on_scalar)
        stage(3, on_vector)
        stage(4, on_scalar)
        scatter_on_scalar(1, 0)
        scatter_on_vector(1, 1)
        scatter_on_scalar(1, 3, 0, 6)
        scatter_on_scalar(0, 2)
        scatter_on_vector(1, 2)
        scatter_on_scalar(0, 3)
        scatter_on_vector(1, 3, 6, LIST_COLS)
        for t in range(2):
            add_taps(t, slice(0, U), nc.gpsimd)
            store_total(t)
        add_taps(2, slice(0, U), nc.vector)
        store_total(2)
        pieces = (slice(0, 192), slice(U // 2, U), slice(192, U // 2))
        for piece in pieces:
            add_taps(3, piece, nc.vector)
        store_total(3)
        group_out(pieces[0], on_scalar)
        group_out(pieces[1], on_vector)
        group_out(pieces[2], on_vector)
        quantize_out(slice(U // 2, U))
        quantize_out(slice(0, U // 2))
        scale_rows = out_2[0].bitcast(I32)
        for q in range(4):
            queue = nc.scalar if q % 2 else nc.sync
            queue.dma_start(scale_rows[4 * q : 4 * q + 4, :], out_scales[32 * q : 32 * q + 4, :].bitcast(I32))
